import numpy as np
import ml_dtypes


def mxq(x, axis, fmt="e4m3"):
    dtype, down = {"e4m3": (ml_dtypes.float8_e4m3fn, 7), "e5m2": (ml_dtypes.float8_e5m2, 14)}[fmt]
    v = np.moveaxis(np.asarray(x, np.float32).astype(ml_dtypes.bfloat16).astype(np.float64), axis, -1)
    blocks = v.reshape(v.shape[:-1] + (-1, 32))
    amax = np.abs(blocks).max(-1, keepdims=True)
    byte = np.maximum(np.where(amax > 0, np.frexp(amax)[1] - 1 + 127, 0) - down, 1)
    scale = np.exp2(byte - 127.0)
    codes = (blocks / scale).astype(np.float32).astype(dtype).astype(np.float64)
    return np.moveaxis((codes * scale).reshape(v.shape), -1, axis)


WIDE = False


def mx_kscale(k):
    if not WIDE:
        return np.ones(k)
    levels = np.array([10, -10, 5, -5, 0])
    if k % 512:
        return np.exp2(np.random.permutation(np.resize(levels, k // 32))).repeat(32)
    a = np.empty((k // 512, 16))
    for p in range(k // 512):
        a[p, :8] = np.random.permutation(np.resize(levels, 8))
        for g in range(8):
            far = levels[np.abs(levels - a[p, g]) >= 10]
            a[p, g + 8] = far[np.random.randint(len(far))]
    return np.exp2(a.ravel()).repeat(32)


def f64(x):
    return np.asarray(x).astype(np.float64)


def striped8(idx):
    return np.asarray(idx).reshape(8, -1, 16).transpose(0, 2, 1).reshape(128, -1).astype(np.uint16)


def unstriped8(offs):
    return offs.reshape(8, 16, -1).transpose(0, 2, 1).reshape(8, -1).astype(np.int64)


def pick8(x, idx, run):
    r = np.arange(len(x))
    return x[r[:, None], idx[r % (8 * run) // run]]


E2M1 = np.array([0.0, 0.5, 1.0, 1.5, 2.0, 3.0, 4.0, 6.0, -0.0, -0.5, -1.0, -1.5, -2.0, -3.0, -4.0, -6.0])


def pack_weight(w, fmt):
    k, n = w.shape
    w = f64(np.asarray(w, np.float32).astype(ml_dtypes.bfloat16)).reshape(k // 32, 32, n)
    amax = np.abs(w).max(1)
    if fmt == "e4m3":
        byte = np.frexp(amax)[1] - 1 + 127 - 7
    else:
        mant, ex = np.frexp(amax / 6.0)
        byte = np.where(mant > 0.5, ex, ex - 1) + 127
    byte = np.clip(np.where(amax > 0, byte, 1), 1, 254)
    scaled = (w * np.exp2(127.0 - byte)[:, None, :]).reshape(k, n).astype(np.float32)
    by_word = np.ascontiguousarray(scaled.reshape(k // 512, 128, 4, n).transpose(0, 1, 3, 2))
    if fmt == "e4m3":
        words = by_word.astype(ml_dtypes.float8_e4m3fn).view(np.uint8)
    else:
        c = by_word.astype(ml_dtypes.float4_e2m1fn).view(np.uint8) & 0xF
        words = (c[..., 0::2] | (c[..., 1::2] << 4)).reshape(k // 512, 128, 2 * n)
    return np.ascontiguousarray(words), np.ascontiguousarray(byte.astype(np.uint8).reshape(k // 512, 16, n))


def unpack_weight(words, scales, fmt):
    g, _, n = scales.shape
    words = np.ascontiguousarray(words).reshape(g, 128, n, -1)
    if fmt == "e4m3":
        vals = words.view(ml_dtypes.float8_e4m3fn).astype(np.float64)
    else:
        nib = np.empty((g, 128, n, 4), np.uint8)
        nib[..., 0::2] = words & 0xF
        nib[..., 1::2] = words >> 4
        vals = E2M1[nib]
    vals = vals * np.repeat(np.exp2(scales.astype(np.float64) - 127.0), 8, axis=1)[..., None]
    return vals.transpose(0, 1, 3, 2).reshape(g * 512, n)


D, T, I, J, P, Q, E = 512, 2048, 512, 256, 512, 512, 256


def setup_inputs():
    n = np.random.standard_normal
    idx = np.stack([np.random.permutation(P)[:J] for _ in range(8)])
    idx2 = np.stack([np.random.permutation(P)[:J] for _ in range(8)])
    idx3 = np.stack([np.random.permutation(P)[:J] for _ in range(8)])
    idx4 = np.stack([np.random.permutation(P)[:J] for _ in range(8)])
    idx5 = np.stack([np.random.permutation(T)[:I] for _ in range(8)])
    idx6 = np.stack([np.random.permutation(T)[:I] for _ in range(8)])
    fd = mx_kscale(D)
    fq = mx_kscale(Q)
    cachep = pack_weight(n((D, T)) / fd[:, None], "e4m3")
    mixp = pack_weight(n((Q, E)) * 1.0 / np.sqrt(Q) / fq[:, None], "e2m1")
    return {
        "query": (n((D, Q)) * 1.0 / np.sqrt(D) * fd[:, None]).astype(np.float32),
        "cache_words": cachep[0],
        "cache_scales": cachep[1],
        "rowf": (np.random.uniform(0.5, 2.0, (Q, 1)) * fq[:, None]).astype(np.float32),
        "mix_words": mixp[0],
        "mix_scales": mixp[1],
        "offs": striped8(idx),
        "offs2": striped8(idx2),
        "offs3": striped8(idx3),
        "offs4": striped8(idx4),
        "offs5": striped8(idx5),
        "offs6": striped8(idx6),
    }


def reference(query, cache_words, cache_scales, rowf, mix_words, mix_scales, offs, offs2, offs3, offs4, offs5, offs6):
    idx = unstriped8(offs)
    idx2 = unstriped8(offs2)
    idx3 = unstriped8(offs3)
    idx4 = unstriped8(offs4)
    idx5 = unstriped8(offs5)
    idx6 = unstriped8(offs6)
    cacheu = unpack_weight(cache_words, cache_scales, "e4m3")
    mixu = unpack_weight(mix_words, mix_scales, "e2m1")
    queryq = mxq(f64(query), 0, "e4m3")
    a = queryq.T @ cacheu
    pm = a.reshape(Q, P, T // P).max(axis=2)
    f1 = np.zeros((Q, P))
    f1[np.arange(Q)[:, None], idx2[np.arange(Q) % 512 // 64]] = pick8(pm, idx, 64)
    bp = pm - f1
    f2 = np.zeros((Q, P))
    f2[np.arange(Q)[:, None], idx4[np.arange(Q) % 512 // 64]] = pick8(bp, idx3, 64)
    b2 = np.maximum(pm, f2)
    sp = np.repeat(b2, T // P, axis=1)
    r = a - sp
    g = np.maximum(pick8(r, idx5, 64), pick8(a, idx6, 64))
    gw = g * f64(rowf)
    gwq = mxq(gw, 0, "e4m3")
    y = mixu.T @ gwq
    return y

@@ -1,0 +1,218 @@
+from contextlib import ExitStack
+
+import concourse.mybir as mybir
+
+F32 = mybir.dt.float32
+BF16 = mybir.dt.bfloat16
+I32 = mybir.dt.int32
+U32 = mybir.dt.uint32
+U16 = mybir.dt.uint16
+U8 = mybir.dt.uint8
+FP8X4 = mybir.dt.float8_e4m3fn_x4
+FP4X4 = mybir.dt.float4_e2m1fn_x4
+ALU = mybir.AluOpType
+COPY = mybir.ActivationFunctionType.Copy
+AX = mybir.AxisListType.X
+
+D, T, SLOTS, PICKS, PAGES, Q, E = 512, 2048, 512, 256, 512, 512, 256
+P = 128
+PACK = 4
+BANK = 512
+CHUNKS = T // BANK
+FLOPS = 2 * D * Q * T + 2 * Q * E * SLOTS
+
+
+def tile_attend_blockmoves_one_mixed_kernel(
+    tc, query, cache_words, cache_scales, rowf, mix_words, mix_scales, offs, offs2, offs3, offs4, offs5, offs6, out
+):
+    nc = tc.nc
+    with ExitStack() as ctx:
+        keep = ctx.enter_context(tc.tile_pool(name="keep", bufs=1))
+        psum = ctx.enter_context(tc.psum_pool(name="psum", bufs=8))
+
+        cache_plane = keep.tile([P, BANK], U8, name="cache_plane", align_bytes=64)
+        nc.vector.memset(cache_plane[:].bitcast(I32), 0)
+        mix_plane = keep.tile([P, E], U8, name="mix_plane", align_bytes=64)
+        nc.vector.memset(mix_plane[:].bitcast(I32), 0)
+
+        halves = 2
+        hw = Q // halves
+        q_rows = query.rearrange("(p j) q -> p j q", j=PACK)
+        q_raw = []
+        for h in range(halves):
+            raw = keep.tile([P, PACK, hw], F32, name=f"q_raw{h}")
+            nc.sync.dma_start(out=raw[:], in_=q_rows[:, :, h * hw : (h + 1) * hw])
+            q_raw.append(raw)
+        scale_rows = cache_scales[0].bitcast(I32)
+        for quad in range(4):
+            nc.sync.dma_start(
+                out=cache_plane[32 * quad : 32 * quad + 16, :].bitcast(I32),
+                in_=scale_rows[4 * quad : 4 * quad + 4, :].rearrange("f (c w) -> c f w", c=CHUNKS),
+            )
+        words = cache_words[0].rearrange("p n t -> p (n t)").bitcast(I32)
+        cache_first = keep.tile([P, BANK], U32, name="cache_first", align_bytes=64)
+        nc.sync.dma_start(out=cache_first[:].bitcast(I32), in_=words[:, 0:BANK])
+        cache_rest = keep.tile([P, T - BANK], U32, name="cache_rest", align_bytes=64)
+        nc.sync.dma_start(out=cache_rest[:].bitcast(I32), in_=words[:, BANK:T])
+        cache_chunks = [cache_first[:]] + [cache_rest[:, c * BANK : (c + 1) * BANK] for c in range(CHUNKS - 1)]
+
+        lists = []
+        for n, src in enumerate((offs, offs2, offs3, offs4, offs5, offs6)):
+            lst = keep.tile(list(src.shape), U16, name=f"list{n}")
+            nc.sync.dma_start(lst[:], src)
+            lists.append(lst)
+        pick_pm, put_f1, pick_bp, put_f2, pick_r, pick_a = lists
+
+        factor = keep.tile([P, PACK], F32, name="factor")
+        nc.sync.dma_start(out=factor[:], in_=rowf.rearrange("(p t) o -> p (t o)", t=PACK))
+        mix_codes = keep.tile([P, 2 * E], U8, name="mix_codes", align_bytes=64)
+        nc.sync.dma_start(out=mix_codes[:].bitcast(I32), in_=mix_words[0].bitcast(I32))
+        mix_rows = mix_scales[0].bitcast(I32)
+        for quad in range(4):
+            nc.sync.dma_start(
+                out=mix_plane[32 * quad : 32 * quad + 4, :].bitcast(I32), in_=mix_rows[4 * quad : 4 * quad + 4, :]
+            )
+
+        f1s, f2s = [], []
+        for t in range(PACK):
+            f1 = keep.tile([P, PAGES], F32, name=f"f1_{t}")
+            nc.vector.memset(f1[:], 0.0)
+            f1s.append(f1)
+        for t in range(PACK):
+            f2 = keep.tile([P, PAGES], F32, name=f"f2_{t}")
+            nc.vector.memset(f2[:], 0.0)
+            f2s.append(f2)
+
+        q_first = keep.tile([P, P, PACK], BF16, name="q_first", align_bytes=64)
+        q_rest = keep.tile([P, PACK - 1, P, PACK], BF16, name="q_rest", align_bytes=64)
+        mh = hw // PACK
+        for h in range(halves):
+            cols = q_raw[h][:].rearrange("p j (m t) -> p m j t", t=PACK)
+            nc.vector.tensor_copy(out=q_first[:, h * mh : (h + 1) * mh, :], in_=cols[:, :, :, 0])
+            nc.scalar.activation(
+                q_rest[:, :, h * mh : (h + 1) * mh, :].rearrange("p t m j -> p m j t"), cols[:, :, :, 1:PACK], COPY
+            )
+        q_codes = keep.tile([P, Q], U32, name="q_codes", align_bytes=64)
+        q_plane = keep.tile([P, Q], U8, name="q_plane", align_bytes=64)
+        for t in range(PACK):
+            q_bf = q_first[:] if t == 0 else q_rest[:, t - 1, :, :]
+            nc.vector.quantize_mx(
+                out=q_codes[:, t * P : (t + 1) * P].bitcast(FP8X4),
+                scales=q_plane[:, t * P : (t + 1) * P],
+                in_=q_bf.rearrange("p m j -> p (m j)"),
+            )
+
+        a, pm, pm_picked, bp_picked, r = {}, {}, {}, {}, {}
+
+        def score(t):
+            a[t] = keep.tile([P, T], F32, name=f"a{t}")
+            for c in range(CHUNKS):
+                acc = psum.tile([P, BANK], F32, name="acc")
+                nc.tensor.matmul_mx(
+                    out=acc[:],
+                    lhsT=q_codes[:, t * P : (t + 1) * P].bitcast(FP8X4),
+                    lhsT_scale=q_plane[:, t * P : (t + 1) * P],
+                    rhs=cache_chunks[c].bitcast(FP8X4),
+                    rhs_scale=cache_plane[4 * c : P, :],
+                    start=True,
+                    stop=True,
+                )
+                if t < 2 and c == CHUNKS - 1:
+                    nc.vector.tensor_copy(a[t][:, c * BANK : (c + 1) * BANK], acc[:])
+                else:
+                    nc.scalar.copy(a[t][:, c * BANK : (c + 1) * BANK], acc[:])
+            a_pages = a[t][:].rearrange("p (g k) -> p g k", k=PACK)
+            pairs = keep.tile([P, PAGES, 2], F32, name=f"pairs{t}")
+            nc.vector.tensor_tensor(pairs[:], a_pages[:, :, 0:2], a_pages[:, :, 2:4], ALU.max)
+            pm[t] = keep.tile([P, PAGES], F32, name=f"pm{t}", tag=f"pages{t}")
+            nc.vector.tensor_tensor(pm[t][:], pairs[:, :, 0], pairs[:, :, 1], ALU.max)
+            pm_picked[t] = keep.tile([P, PICKS], F32, name=f"pm_picked{t}")
+            nc.vector.tensor_copy(pm_picked[t][:], pm[t][:].indirect(pick_pm[:]))
+
+        def first_move(t):
+            nc.scalar.activation(f1s[t][:].indirect(put_f1[:]), pm_picked[t][:], COPY)
+            bp = keep.tile([P, PAGES], F32, name=f"bp{t}")
+            nc.vector.tensor_tensor(bp[:], pm[t][:], f1s[t][:], ALU.subtract)
+            bp_picked[t] = keep.tile([P, PICKS], F32, name=f"bp_picked{t}")
+            nc.vector.tensor_copy(bp_picked[t][:], bp[:].indirect(pick_bp[:]))
+
+        def second_move(t):
+            nc.scalar.activation(f2s[t][:].indirect(put_f2[:]), bp_picked[t][:], COPY)
+            b2 = keep.tile([P, PAGES], F32, name=f"b2{t}")
+            nc.vector.tensor_tensor(b2[:], pm[t][:], f2s[t][:], ALU.max)
+            r[t] = keep.tile([P, T], F32, name=f"r{t}")
+            nc.vector.tensor_tensor(
+                r[t][:].rearrange("p (g k) -> p g k", k=PACK),
+                a[t][:].rearrange("p (g k) -> p g k", k=PACK),
+                b2[:].unsqueeze(2).to_broadcast([P, PAGES, PACK]),
+                ALU.subtract,
+            )
+
+        gw_pairs = keep.tile([P, 2, SLOTS, 2], BF16, name="gw_pairs")
+        sh = SLOTS // halves
+
+        def weigh(t):
+            a_picked = keep.tile([P, SLOTS], F32, name=f"a_picked{t}", tag=f"pages{t}")
+            if t == 0:
+                nc.vector.tensor_copy(a_picked[:], a[t][:].indirect(pick_a[:]))
+            else:
+                nc.scalar.activation(a_picked[:], a[t][:].indirect(pick_a[:]), COPY)
+            r_picked = keep.tile([P, SLOTS], F32, name=f"r_picked{t}")
+            nc.scalar.activation(r_picked[:], r[t][:].indirect(pick_r[:]), COPY)
+            g = keep.tile([P, SLOTS], F32, name=f"g{t}")
+            parts = [slice(h * sh, (h + 1) * sh) for h in range(halves)] if t == PACK - 1 else [slice(0, SLOTS)]
+            for part in parts:
+                nc.vector.tensor_tensor(g[:, part], r_picked[:, part], a_picked[:, part], ALU.max)
+            for part in parts:
+                if t < 2:
+                    nc.scalar.activation(gw_pairs[:, 0, part, t], g[:, part], COPY, scale=factor[:, t : t + 1])
+                else:
+                    nc.vector.tensor_scalar(gw_pairs[:, 1, part, t - 2], g[:, part], factor[:, t : t + 1], None, ALU.mult)
+
+        for t in range(PACK):
+            score(t)
+        lag = 3
+        for step in range(PACK + lag):
+            if step >= lag:
+                second_move(step - lag)
+            if step < PACK:
+                first_move(step)
+        for t in range(PACK):
+            weigh(t)
+
+        pair_words = gw_pairs[:].rearrange("p u i k -> p u (i k)").bitcast(F32).rearrange("p u i -> p i u")
+        gw = []
+        for h in range(halves):
+            gw_h = keep.tile([P, sh * PACK], BF16, name=f"gw{h}", align_bytes=64)
+            gw_words = gw_h[:].bitcast(F32).rearrange("p (i u) -> p i u", u=2)
+            if h == 0:
+                nc.vector.tensor_copy(gw_words, pair_words[:, h * sh : (h + 1) * sh, :])
+            else:
+                nc.scalar.copy(gw_words, pair_words[:, h * sh : (h + 1) * sh, :])
+            gw.append(gw_h)
+        gw_codes, gw_plane = [], []
+        for h in range(halves):
+            codes = keep.tile([P, sh], U32, name=f"gw_codes{h}", align_bytes=64)
+            plane = keep.tile([P, sh], U8, name=f"gw_plane{h}", align_bytes=64)
+            nc.vector.quantize_mx(out=codes[:].bitcast(FP8X4), scales=plane[:], in_=gw[h][:])
+            gw_codes.append(codes)
+            gw_plane.append(plane)
+        out_rows = out.rearrange("(e p) i -> p e i", p=P)
+        for h in range(halves):
+            y = keep.tile([P, E // P, sh], F32, name=f"y{h}")
+            for e in range(E // P):
+                acc = psum.tile([P, sh], F32, name="acc")
+                nc.tensor.matmul_mx(
+                    out=acc[:],
+                    lhsT=mix_codes[:, 2 * P * e : 2 * P * (e + 1)].bitcast(FP4X4),
+                    lhsT_scale=mix_plane[:, P * e : P * (e + 1)],
+                    rhs=gw_codes[h][:].bitcast(FP8X4),
+                    rhs_scale=gw_plane[h][:],
+                    start=True,
+                    stop=True,
+                )
+                if e == 0:
+                    nc.scalar.copy(y[:, e, :], acc[:])
+                else:
+                    nc.vector.tensor_copy(y[:, e, :], acc[:])
+            nc.sync.dma_start(out=out_rows[:, :, h * sh : (h + 1) * sh], in_=y[:])

@@ -50,11 +50,11 @@ def tile_attend_blockmoves_one_mixed_kernel(
                 in_=scale_rows[4 * quad : 4 * quad + 4, :].rearrange("f (c w) -> c f w", c=CHUNKS),
             )
         words = cache_words[0].rearrange("p n t -> p (n t)").bitcast(I32)
-        cache_first = keep.tile([P, BANK], U32, name="cache_first", align_bytes=64)
-        nc.sync.dma_start(out=cache_first[:].bitcast(I32), in_=words[:, 0:BANK])
-        cache_rest = keep.tile([P, T - BANK], U32, name="cache_rest", align_bytes=64)
-        nc.sync.dma_start(out=cache_rest[:].bitcast(I32), in_=words[:, BANK:T])
-        cache_chunks = [cache_first[:]] + [cache_rest[:, c * BANK : (c + 1) * BANK] for c in range(CHUNKS - 1)]
+        cache_chunks = []
+        for c in range(CHUNKS):
+            chunk = keep.tile([P, BANK], U32, name=f"cache{c}", align_bytes=64)
+            nc.sync.dma_start(out=chunk[:].bitcast(I32), in_=words[:, c * BANK : (c + 1) * BANK])
+            cache_chunks.append(chunk[:])
 
         lists = []
         for n, src in enumerate((offs, offs2, offs3, offs4, offs5, offs6)):
@@ -74,13 +74,13 @@ def tile_attend_blockmoves_one_mixed_kernel(
             )
 
         f1s, f2s = [], []
-        for t in range(PACK):
+        for t in range(2):
             f1 = keep.tile([P, PAGES], F32, name=f"f1_{t}")
-            nc.vector.memset(f1[:], 0.0)
+            nc.gpsimd.memset(f1[:], 0.0)
             f1s.append(f1)
-        for t in range(PACK):
+        for t in range(2):
             f2 = keep.tile([P, PAGES], F32, name=f"f2_{t}")
-            nc.vector.memset(f2[:], 0.0)
+            nc.gpsimd.memset(f2[:], 0.0)
             f2s.append(f2)
 
         q_first = keep.tile([P, P, PACK], BF16, name="q_first", align_bytes=64)
@@ -102,12 +102,13 @@ def tile_attend_blockmoves_one_mixed_kernel(
                 in_=q_bf.rearrange("p m j -> p (m j)"),
             )
 
-        a, pm, pm_picked, bp_picked, r = {}, {}, {}, {}, {}
+        a, banks, pm, pm_picked, bp_picked, r = {}, {}, {}, {}, {}, {}
 
         def score(t):
             a[t] = keep.tile([P, T], F32, name=f"a{t}")
             for c in range(CHUNKS):
                 acc = psum.tile([P, BANK], F32, name="acc")
+                banks[t, c] = acc
                 nc.tensor.matmul_mx(
                     out=acc[:],
                     lhsT=q_codes[:, t * P : (t + 1) * P].bitcast(FP8X4),
@@ -117,36 +118,48 @@ def tile_attend_blockmoves_one_mixed_kernel(
                     start=True,
                     stop=True,
                 )
-                if t < 2 and c == CHUNKS - 1:
+                if (t == 0 and c == 1) or (t < 2 and c == CHUNKS - 1):
                     nc.vector.tensor_copy(a[t][:, c * BANK : (c + 1) * BANK], acc[:])
                 else:
                     nc.scalar.copy(a[t][:, c * BANK : (c + 1) * BANK], acc[:])
             a_pages = a[t][:].rearrange("p (g k) -> p g k", k=PACK)
             pairs = keep.tile([P, PAGES, 2], F32, name=f"pairs{t}")
-            nc.vector.tensor_tensor(pairs[:], a_pages[:, :, 0:2], a_pages[:, :, 2:4], ALU.max)
+            parts = [slice(0, PAGES // 2), slice(PAGES // 2, PAGES)] if t == 0 else [slice(0, PAGES)]
+            for part in parts:
+                nc.vector.tensor_tensor(pairs[:, part, :], a_pages[:, part, 0:2], a_pages[:, part, 2:4], ALU.max)
             pm[t] = keep.tile([P, PAGES], F32, name=f"pm{t}", tag=f"pages{t}")
             nc.vector.tensor_tensor(pm[t][:], pairs[:, :, 0], pairs[:, :, 1], ALU.max)
             pm_picked[t] = keep.tile([P, PICKS], F32, name=f"pm_picked{t}")
             nc.vector.tensor_copy(pm_picked[t][:], pm[t][:].indirect(pick_pm[:]))
 
         def first_move(t):
-            nc.scalar.activation(f1s[t][:].indirect(put_f1[:]), pm_picked[t][:], COPY)
+            nc.scalar.activation(f1s[t % 2][:].indirect(put_f1[:]), pm_picked[t][:], COPY)
             bp = keep.tile([P, PAGES], F32, name=f"bp{t}")
-            nc.vector.tensor_tensor(bp[:], pm[t][:], f1s[t][:], ALU.subtract)
+            nc.vector.tensor_tensor(bp[:], pm[t][:], f1s[t % 2][:], ALU.subtract)
             bp_picked[t] = keep.tile([P, PICKS], F32, name=f"bp_picked{t}")
             nc.vector.tensor_copy(bp_picked[t][:], bp[:].indirect(pick_bp[:]))
 
         def second_move(t):
-            nc.scalar.activation(f2s[t][:].indirect(put_f2[:]), bp_picked[t][:], COPY)
+            nc.scalar.activation(f2s[t % 2][:].indirect(put_f2[:]), bp_picked[t][:], COPY)
             b2 = keep.tile([P, PAGES], F32, name=f"b2{t}")
-            nc.vector.tensor_tensor(b2[:], pm[t][:], f2s[t][:], ALU.max)
+            nc.vector.tensor_tensor(b2[:], pm[t][:], f2s[t % 2][:], ALU.max)
             r[t] = keep.tile([P, T], F32, name=f"r{t}")
-            nc.vector.tensor_tensor(
-                r[t][:].rearrange("p (g k) -> p g k", k=PACK),
-                a[t][:].rearrange("p (g k) -> p g k", k=PACK),
-                b2[:].unsqueeze(2).to_broadcast([P, PAGES, PACK]),
-                ALU.subtract,
-            )
+            r_pages = r[t][:].rearrange("p (g k) -> p g k", k=PACK)
+            a_pages = a[t][:].rearrange("p (g k) -> p g k", k=PACK)
+            if t < 2:
+                nc.vector.tensor_tensor(
+                    r_pages, a_pages, b2[:].unsqueeze(2).to_broadcast([P, PAGES, PACK]), ALU.subtract
+                )
+            else:
+                pb = BANK // PACK
+                for c in range(CHUNKS):
+                    pages = slice(c * pb, (c + 1) * pb)
+                    marks = b2[:, pages].unsqueeze(2).to_broadcast([P, pb, PACK])
+                    if c == 0:
+                        nc.gpsimd.tensor_tensor(r_pages[:, pages, :], a_pages[:, pages, :], marks, ALU.subtract)
+                    else:
+                        scores = banks[t, c][:].rearrange("p (g k) -> p g k", k=PACK)
+                        nc.vector.tensor_tensor(r_pages[:, pages, :], scores, marks, ALU.subtract)
 
         gw_pairs = keep.tile([P, 2, SLOTS, 2], BF16, name="gw_pairs")
         sh = SLOTS // halves

@@ -33,7 +33,6 @@ def tile_attend_blockmoves_one_mixed_kernel(
         cache_plane = keep.tile([P, BANK], U8, name="cache_plane", align_bytes=64)
         nc.vector.memset(cache_plane[:].bitcast(I32), 0)
         mix_plane = keep.tile([P, E], U8, name="mix_plane", align_bytes=64)
-        nc.vector.memset(mix_plane[:].bitcast(I32), 0)
 
         halves = 2
         hw = Q // halves
@@ -44,17 +43,18 @@ def tile_attend_blockmoves_one_mixed_kernel(
             nc.sync.dma_start(out=raw[:], in_=q_rows[:, :, h * hw : (h + 1) * hw])
             q_raw.append(raw)
         scale_rows = cache_scales[0].bitcast(I32)
-        for quad in range(4):
-            nc.sync.dma_start(
-                out=cache_plane[32 * quad : 32 * quad + 16, :].bitcast(I32),
-                in_=scale_rows[4 * quad : 4 * quad + 4, :].rearrange("f (c w) -> c f w", c=CHUNKS),
-            )
         words = cache_words[0].rearrange("p n t -> p (n t)").bitcast(I32)
         cache_chunks = []
         for c in range(CHUNKS):
             chunk = keep.tile([P, BANK], U32, name=f"cache{c}", align_bytes=64)
             nc.sync.dma_start(out=chunk[:].bitcast(I32), in_=words[:, c * BANK : (c + 1) * BANK])
             cache_chunks.append(chunk[:])
+            if c == 0:
+                for quad in range(4):
+                    nc.sync.dma_start(
+                        out=cache_plane[32 * quad : 32 * quad + 16, :].bitcast(I32),
+                        in_=scale_rows[4 * quad : 4 * quad + 4, :].rearrange("f (c w) -> c f w", c=CHUNKS),
+                    )
 
         lists = []
         for n, src in enumerate((offs, offs2, offs3, offs4, offs5, offs6)):
@@ -67,6 +67,7 @@ def tile_attend_blockmoves_one_mixed_kernel(
         nc.sync.dma_start(out=factor[:], in_=rowf.rearrange("(p t) o -> p (t o)", t=PACK))
         mix_codes = keep.tile([P, 2 * E], U8, name="mix_codes", align_bytes=64)
         nc.sync.dma_start(out=mix_codes[:].bitcast(I32), in_=mix_words[0].bitcast(I32))
+        nc.gpsimd.memset(mix_plane[:].bitcast(I32), 0)
         mix_rows = mix_scales[0].bitcast(I32)
         for quad in range(4):
             nc.sync.dma_start(
@@ -118,13 +119,13 @@ def tile_attend_blockmoves_one_mixed_kernel(
                     start=True,
                     stop=True,
                 )
-                if (t == 0 and c == 1) or (t < 2 and c == CHUNKS - 1):
+                if t < 2 and c == CHUNKS - 1:
                     nc.vector.tensor_copy(a[t][:, c * BANK : (c + 1) * BANK], acc[:])
                 else:
                     nc.scalar.copy(a[t][:, c * BANK : (c + 1) * BANK], acc[:])
             a_pages = a[t][:].rearrange("p (g k) -> p g k", k=PACK)
             pairs = keep.tile([P, PAGES, 2], F32, name=f"pairs{t}")
-            parts = [slice(0, PAGES // 2), slice(PAGES // 2, PAGES)] if t == 0 else [slice(0, PAGES)]
+            parts = [slice(0, PAGES // 2), slice(PAGES // 2, PAGES)]
             for part in parts:
                 nc.vector.tensor_tensor(pairs[:, part, :], a_pages[:, part, 0:2], a_pages[:, part, 2:4], ALU.max)
             pm[t] = keep.tile([P, PAGES], F32, name=f"pm{t}", tag=f"pages{t}")
@@ -171,7 +172,10 @@ def tile_attend_blockmoves_one_mixed_kernel(
             else:
                 nc.scalar.activation(a_picked[:], a[t][:].indirect(pick_a[:]), COPY)
             r_picked = keep.tile([P, SLOTS], F32, name=f"r_picked{t}")
-            nc.scalar.activation(r_picked[:], r[t][:].indirect(pick_r[:]), COPY)
+            if t == PACK - 1:
+                nc.vector.tensor_copy(r_picked[:], r[t][:].indirect(pick_r[:]))
+            else:
+                nc.scalar.activation(r_picked[:], r[t][:].indirect(pick_r[:]), COPY)
             g = keep.tile([P, SLOTS], F32, name=f"g{t}")
             parts = [slice(h * sh, (h + 1) * sh) for h in range(halves)] if t == PACK - 1 else [slice(0, SLOTS)]
             for part in parts:
@@ -210,9 +214,7 @@ def tile_attend_blockmoves_one_mixed_kernel(
             nc.vector.quantize_mx(out=codes[:].bitcast(FP8X4), scales=plane[:], in_=gw[h][:])
             gw_codes.append(codes)
             gw_plane.append(plane)
-        out_rows = out.rearrange("(e p) i -> p e i", p=P)
         for h in range(halves):
-            y = keep.tile([P, E // P, sh], F32, name=f"y{h}")
             for e in range(E // P):
                 acc = psum.tile([P, sh], F32, name="acc")
                 nc.tensor.matmul_mx(
@@ -224,8 +226,9 @@ def tile_attend_blockmoves_one_mixed_kernel(
                     start=True,
                     stop=True,
                 )
+                y = keep.tile([P, sh], F32, name=f"y{h}{e}")
                 if e == 0:
-                    nc.scalar.copy(y[:, e, :], acc[:])
+                    nc.scalar.copy(y[:], acc[:])
                 else:
-                    nc.vector.tensor_copy(y[:, e, :], acc[:])
-            nc.sync.dma_start(out=out_rows[:, :, h * sh : (h + 1) * sh], in_=y[:])
+                    nc.vector.tensor_copy(y[:], acc[:])
+                nc.sync.dma_start(out=out[P * e : P * (e + 1), h * sh : (h + 1) * sh], in_=y[:])

@@ -84,24 +84,23 @@ def tile_attend_blockmoves_one_mixed_kernel(
             nc.gpsimd.memset(f2[:], 0.0)
             f2s.append(f2)
 
-        q_first = keep.tile([P, P, PACK], BF16, name="q_first", align_bytes=64)
-        q_rest = keep.tile([P, PACK - 1, P, PACK], BF16, name="q_rest", align_bytes=64)
         mh = hw // PACK
-        for h in range(halves):
-            cols = q_raw[h][:].rearrange("p j (m t) -> p m j t", t=PACK)
-            nc.vector.tensor_copy(out=q_first[:, h * mh : (h + 1) * mh, :], in_=cols[:, :, :, 0])
-            nc.scalar.activation(
-                q_rest[:, :, h * mh : (h + 1) * mh, :].rearrange("p t m j -> p m j t"), cols[:, :, :, 1:PACK], COPY
-            )
+        q_bf = [keep.tile([P, P, PACK], BF16, name=f"q_bf{t}", align_bytes=64) for t in range(PACK)]
         q_codes = keep.tile([P, Q], U32, name="q_codes", align_bytes=64)
         q_plane = keep.tile([P, Q], U8, name="q_plane", align_bytes=64)
-        for t in range(PACK):
-            q_bf = q_first[:] if t == 0 else q_rest[:, t - 1, :, :]
-            nc.vector.quantize_mx(
-                out=q_codes[:, t * P : (t + 1) * P].bitcast(FP8X4),
-                scales=q_plane[:, t * P : (t + 1) * P],
-                in_=q_bf.rearrange("p m j -> p (m j)"),
-            )
+        for h in range(halves):
+            cols = q_raw[h][:].rearrange("p j (m t) -> p t m j", t=PACK)
+            for t in range(PACK):
+                if h == 0 and t >= 2:
+                    nc.scalar.copy(q_bf[t][:, h * mh : (h + 1) * mh, :], cols[:, t, :, :])
+                else:
+                    nc.vector.tensor_copy(out=q_bf[t][:, h * mh : (h + 1) * mh, :], in_=cols[:, t, :, :])
+                if h == halves - 1:
+                    nc.vector.quantize_mx(
+                        out=q_codes[:, t * P : (t + 1) * P].bitcast(FP8X4),
+                        scales=q_plane[:, t * P : (t + 1) * P],
+                        in_=q_bf[t][:].rearrange("p m j -> p (m j)"),
+                    )
 
         a, banks, pm, pm_picked, bp_picked, r = {}, {}, {}, {}, {}, {}
 
@@ -172,10 +171,7 @@ def tile_attend_blockmoves_one_mixed_kernel(
             else:
                 nc.scalar.activation(a_picked[:], a[t][:].indirect(pick_a[:]), COPY)
             r_picked = keep.tile([P, SLOTS], F32, name=f"r_picked{t}")
-            if t == PACK - 1:
-                nc.vector.tensor_copy(r_picked[:], r[t][:].indirect(pick_r[:]))
-            else:
-                nc.scalar.activation(r_picked[:], r[t][:].indirect(pick_r[:]), COPY)
+            nc.scalar.activation(r_picked[:], r[t][:].indirect(pick_r[:]), COPY)
             g = keep.tile([P, SLOTS], F32, name=f"g{t}")
             parts = [slice(h * sh, (h + 1) * sh) for h in range(halves)] if t == PACK - 1 else [slice(0, SLOTS)]
             for part in parts:

from contextlib import ExitStack

import concourse.mybir as mybir

F32 = mybir.dt.float32
BF16 = mybir.dt.bfloat16
I32 = mybir.dt.int32
U32 = mybir.dt.uint32
U16 = mybir.dt.uint16
U8 = mybir.dt.uint8
FP8X4 = mybir.dt.float8_e4m3fn_x4
FP4X4 = mybir.dt.float4_e2m1fn_x4
ALU = mybir.AluOpType
COPY = mybir.ActivationFunctionType.Copy
AX = mybir.AxisListType.X

D, T, SLOTS, PICKS, PAGES, Q, E = 512, 2048, 512, 256, 512, 512, 256
P = 128
PACK = 4
BANK = 512
CHUNKS = T // BANK
FLOPS = 2 * D * Q * T + 2 * Q * E * SLOTS


def tile_attend_blockmoves_one_mixed_kernel(
    tc, query, cache_words, cache_scales, rowf, mix_words, mix_scales, offs, offs2, offs3, offs4, offs5, offs6, out
):
    nc = tc.nc
    with ExitStack() as ctx:
        keep = ctx.enter_context(tc.tile_pool(name="keep", bufs=1))
        psum = ctx.enter_context(tc.psum_pool(name="psum", bufs=8))

        cache_plane = keep.tile([P, BANK], U8, name="cache_plane", align_bytes=64)
        nc.vector.memset(cache_plane[:].bitcast(I32), 0)
        mix_plane = keep.tile([P, E], U8, name="mix_plane", align_bytes=64)

        halves = 2
        hw = Q // halves
        q_rows = query.rearrange("(p j) q -> p j q", j=PACK)
        q_raw = []
        for h in range(halves):
            raw = keep.tile([P, PACK, hw], F32, name=f"q_raw{h}")
            nc.sync.dma_start(out=raw[:], in_=q_rows[:, :, h * hw : (h + 1) * hw])
            q_raw.append(raw)
        scale_rows = cache_scales[0].bitcast(I32)
        words = cache_words[0].rearrange("p n t -> p (n t)").bitcast(I32)
        cache_chunks = []
        for c in range(CHUNKS):
            chunk = keep.tile([P, BANK], U32, name=f"cache{c}", align_bytes=64)
            nc.sync.dma_start(out=chunk[:].bitcast(I32), in_=words[:, c * BANK : (c + 1) * BANK])
            cache_chunks.append(chunk[:])
            if c == 0:
                for quad in range(4):
                    nc.sync.dma_start(
                        out=cache_plane[32 * quad : 32 * quad + 16, :].bitcast(I32),
                        in_=scale_rows[4 * quad : 4 * quad + 4, :].rearrange("f (c w) -> c f w", c=CHUNKS),
                    )

        lists = []
        for n, src in enumerate((offs, offs2, offs3, offs4, offs5, offs6)):
            lst = keep.tile(list(src.shape), U16, name=f"list{n}")
            nc.sync.dma_start(lst[:], src)
            lists.append(lst)
        pick_pm, put_f1, pick_bp, put_f2, pick_r, pick_a = lists

        factor = keep.tile([P, PACK], F32, name="factor")
        nc.sync.dma_start(out=factor[:], in_=rowf.rearrange("(p t) o -> p (t o)", t=PACK))
        mix_codes = keep.tile([P, 2 * E], U8, name="mix_codes", align_bytes=64)
        nc.sync.dma_start(out=mix_codes[:].bitcast(I32), in_=mix_words[0].bitcast(I32))
        nc.gpsimd.memset(mix_plane[:].bitcast(I32), 0)
        mix_rows = mix_scales[0].bitcast(I32)
        for quad in range(4):
            nc.sync.dma_start(
                out=mix_plane[32 * quad : 32 * quad + 4, :].bitcast(I32), in_=mix_rows[4 * quad : 4 * quad + 4, :]
            )

        f1s, f2s = [], []
        for t in range(2):
            f1 = keep.tile([P, PAGES], F32, name=f"f1_{t}")
            nc.gpsimd.memset(f1[:], 0.0)
            f1s.append(f1)
        for t in range(2):
            f2 = keep.tile([P, PAGES], F32, name=f"f2_{t}")
            nc.gpsimd.memset(f2[:], 0.0)
            f2s.append(f2)

        mh = hw // PACK
        q_bf = [keep.tile([P, P, PACK], BF16, name=f"q_bf{t}", align_bytes=64) for t in range(PACK)]
        q_codes = keep.tile([P, Q], U32, name="q_codes", align_bytes=64)
        q_plane = keep.tile([P, Q], U8, name="q_plane", align_bytes=64)
        for h in range(halves):
            cols = q_raw[h][:].rearrange("p j (m t) -> p t m j", t=PACK)
            for t in range(PACK):
                if h == 0 and t >= 2:
                    nc.scalar.copy(q_bf[t][:, h * mh : (h + 1) * mh, :], cols[:, t, :, :])
                else:
                    nc.vector.tensor_copy(out=q_bf[t][:, h * mh : (h + 1) * mh, :], in_=cols[:, t, :, :])
                if h == halves - 1:
                    nc.vector.quantize_mx(
                        out=q_codes[:, t * P : (t + 1) * P].bitcast(FP8X4),
                        scales=q_plane[:, t * P : (t + 1) * P],
                        in_=q_bf[t][:].rearrange("p m j -> p (m j)"),
                    )

        a, banks, pm, pm_picked, bp_picked, r = {}, {}, {}, {}, {}, {}

        def score(t):
            a[t] = keep.tile([P, T], F32, name=f"a{t}")
            for c in range(CHUNKS):
                acc = psum.tile([P, BANK], F32, name="acc")
                banks[t, c] = acc
                nc.tensor.matmul_mx(
                    out=acc[:],
                    lhsT=q_codes[:, t * P : (t + 1) * P].bitcast(FP8X4),
                    lhsT_scale=q_plane[:, t * P : (t + 1) * P],
                    rhs=cache_chunks[c].bitcast(FP8X4),
                    rhs_scale=cache_plane[4 * c : P, :],
                    start=True,
                    stop=True,
                )
                if t < 2 and c == CHUNKS - 1:
                    nc.vector.tensor_copy(a[t][:, c * BANK : (c + 1) * BANK], acc[:])
                else:
                    nc.scalar.copy(a[t][:, c * BANK : (c + 1) * BANK], acc[:])
            a_pages = a[t][:].rearrange("p (g k) -> p g k", k=PACK)
            pairs = keep.tile([P, PAGES, 2], F32, name=f"pairs{t}")
            parts = [slice(0, PAGES // 2), slice(PAGES // 2, PAGES)]
            for part in parts:
                nc.vector.tensor_tensor(pairs[:, part, :], a_pages[:, part, 0:2], a_pages[:, part, 2:4], ALU.max)
            pm[t] = keep.tile([P, PAGES], F32, name=f"pm{t}", tag=f"pages{t}")
            nc.vector.tensor_tensor(pm[t][:], pairs[:, :, 0], pairs[:, :, 1], ALU.max)
            pm_picked[t] = keep.tile([P, PICKS], F32, name=f"pm_picked{t}")
            nc.vector.tensor_copy(pm_picked[t][:], pm[t][:].indirect(pick_pm[:]))

        def first_move(t):
            nc.scalar.activation(f1s[t % 2][:].indirect(put_f1[:]), pm_picked[t][:], COPY)
            bp = keep.tile([P, PAGES], F32, name=f"bp{t}")
            nc.vector.tensor_tensor(bp[:], pm[t][:], f1s[t % 2][:], ALU.subtract)
            bp_picked[t] = keep.tile([P, PICKS], F32, name=f"bp_picked{t}")
            nc.vector.tensor_copy(bp_picked[t][:], bp[:].indirect(pick_bp[:]))

        def second_move(t):
            nc.scalar.activation(f2s[t % 2][:].indirect(put_f2[:]), bp_picked[t][:], COPY)
            b2 = keep.tile([P, PAGES], F32, name=f"b2{t}")
            nc.vector.tensor_tensor(b2[:], pm[t][:], f2s[t % 2][:], ALU.max)
            r[t] = keep.tile([P, T], F32, name=f"r{t}")
            r_pages = r[t][:].rearrange("p (g k) -> p g k", k=PACK)
            a_pages = a[t][:].rearrange("p (g k) -> p g k", k=PACK)
            if t < 2:
                nc.vector.tensor_tensor(
                    r_pages, a_pages, b2[:].unsqueeze(2).to_broadcast([P, PAGES, PACK]), ALU.subtract
                )
            else:
                pb = BANK // PACK
                for c in range(CHUNKS):
                    pages = slice(c * pb, (c + 1) * pb)
                    marks = b2[:, pages].unsqueeze(2).to_broadcast([P, pb, PACK])
                    if c == 0:
                        nc.gpsimd.tensor_tensor(r_pages[:, pages, :], a_pages[:, pages, :], marks, ALU.subtract)
                    else:
                        scores = banks[t, c][:].rearrange("p (g k) -> p g k", k=PACK)
                        nc.vector.tensor_tensor(r_pages[:, pages, :], scores, marks, ALU.subtract)

        gw_pairs = keep.tile([P, 2, SLOTS, 2], BF16, name="gw_pairs")
        sh = SLOTS // halves

        def weigh(t):
            a_picked = keep.tile([P, SLOTS], F32, name=f"a_picked{t}", tag=f"pages{t}")
            if t == 0:
                nc.vector.tensor_copy(a_picked[:], a[t][:].indirect(pick_a[:]))
            else:
                nc.scalar.activation(a_picked[:], a[t][:].indirect(pick_a[:]), COPY)
            r_picked = keep.tile([P, SLOTS], F32, name=f"r_picked{t}")
            nc.scalar.activation(r_picked[:], r[t][:].indirect(pick_r[:]), COPY)
            g = keep.tile([P, SLOTS], F32, name=f"g{t}")
            parts = [slice(h * sh, (h + 1) * sh) for h in range(halves)] if t == PACK - 1 else [slice(0, SLOTS)]
            for part in parts:
                nc.vector.tensor_tensor(g[:, part], r_picked[:, part], a_picked[:, part], ALU.max)
            for part in parts:
                if t < 2:
                    nc.scalar.activation(gw_pairs[:, 0, part, t], g[:, part], COPY, scale=factor[:, t : t + 1])
                else:
                    nc.vector.tensor_scalar(gw_pairs[:, 1, part, t - 2], g[:, part], factor[:, t : t + 1], None, ALU.mult)

        for t in range(PACK):
            score(t)
        lag = 3
        for step in range(PACK + lag):
            if step >= lag:
                second_move(step - lag)
            if step < PACK:
                first_move(step)
        for t in range(PACK):
            weigh(t)

        pair_words = gw_pairs[:].rearrange("p u i k -> p u (i k)").bitcast(F32).rearrange("p u i -> p i u")
        gw = []
        for h in range(halves):
            gw_h = keep.tile([P, sh * PACK], BF16, name=f"gw{h}", align_bytes=64)
            gw_words = gw_h[:].bitcast(F32).rearrange("p (i u) -> p i u", u=2)
            if h == 0:
                nc.vector.tensor_copy(gw_words, pair_words[:, h * sh : (h + 1) * sh, :])
            else:
                nc.scalar.copy(gw_words, pair_words[:, h * sh : (h + 1) * sh, :])
            gw.append(gw_h)
        gw_codes, gw_plane = [], []
        for h in range(halves):
            codes = keep.tile([P, sh], U32, name=f"gw_codes{h}", align_bytes=64)
            plane = keep.tile([P, sh], U8, name=f"gw_plane{h}", align_bytes=64)
            nc.vector.quantize_mx(out=codes[:].bitcast(FP8X4), scales=plane[:], in_=gw[h][:])
            gw_codes.append(codes)
            gw_plane.append(plane)
        for h in range(halves):
            for e in range(E // P):
                acc = psum.tile([P, sh], F32, name="acc")
                nc.tensor.matmul_mx(
                    out=acc[:],
                    lhsT=mix_codes[:, 2 * P * e : 2 * P * (e + 1)].bitcast(FP4X4),
                    lhsT_scale=mix_plane[:, P * e : P * (e + 1)],
                    rhs=gw_codes[h][:].bitcast(FP8X4),
                    rhs_scale=gw_plane[h][:],
                    start=True,
                    stop=True,
                )
                y = keep.tile([P, sh], F32, name=f"y{h}{e}")
                if e == 0:
                    nc.scalar.copy(y[:], acc[:])
                else:
                    nc.vector.tensor_copy(y[:], acc[:])
                nc.sync.dma_start(out=out[P * e : P * (e + 1), h * sh : (h + 1) * sh], in_=y[:])
